import numpy as np, ml_dtypes
CORES = [0,8,16,24,32,40,48,56,64,72,80,88,96,104,112,120,128,136,144,152,160,168,176,184,192,200,208,216,224,232,240,248]
N = 32
KT, M, NO = 4, 128, 256
def setup_inputs(rng):
    return {"a": rng.standard_normal((N, 128, KT * M), dtype=np.float32).astype(ml_dtypes.bfloat16), "w": rng.standard_normal((N, 128, KT * NO), dtype=np.float32).astype(ml_dtypes.bfloat16)}
def reference(a, w):
    A = a.astype(np.float64).reshape(N, 128 * KT, M)
    y = []
    for r in range(N):
        W = w[r].astype(np.float64).reshape(128 * KT, NO)
        y.append(np.concatenate([A[j].T @ W for j in range(N)], axis=1))
    return {"y": np.stack(y).astype(ml_dtypes.bfloat16 if a.dtype != np.float64 else np.float64)}

@@ -1,0 +1,96 @@
+import concourse.bass as bass
+
+NR, BW, NO, KT = 32, 512, 256, 4
+NBANK = 8
+SCRATCH = {
+    "ag": ("sbuf", [128, NR * BW], "bfloat16"),
+    "wt": ("sbuf", [128, KT * NO], "bfloat16"),
+    "yo": ("sbuf", [128, NR * NO], "bfloat16"),
+    "acc": ("psum", [128, NBANK * 512], "float32"),
+}
+SEMAPHORES = ["arr%d" % j for j in range(NR)] + ["lda", "ldw", "sent", "mm", "cp", "st"]
+
+OFF = 0x00FF
+
+
+def rank_program(g, core, T, topo):
+    s = T.sem
+    arr = [s.arr0, s.arr1, s.arr2, s.arr3, s.arr4, s.arr5, s.arr6, s.arr7,
+           s.arr8, s.arr9, s.arr10, s.arr11, s.arr12, s.arr13, s.arr14, s.arr15,
+           s.arr16, s.arr17, s.arr18, s.arr19, s.arr20, s.arr21, s.arr22, s.arr23,
+           s.arr24, s.arr25, s.arr26, s.arr27, s.arr28, s.arr29, s.arr30, s.arr31]
+    h, c, l = topo.host(core), topo.chip(core), core % 8
+
+    def wc(hh, cc, ll):
+        return 128 * hh + 8 * (cc % 16) + ll
+
+    def blk(hh, cc):
+        return T.rank_of(wc(hh, cc, 0))
+
+    def a_of(j):
+        return T.ag[:, BW * j:BW * (j + 1)]
+
+    def send(j, dsts):
+        ids = []
+        for d in dsts:
+            rid, pid = topo.addr(d, core)
+            ids.append(bass.DstId(rid=rid, pnc=pid))
+        g.remote_dma_fused([bass.RemoteDMATransfer(dst_ids=ids, dma_engine_mask=OFF, remote_sem=arr[j],
+                                                   src=a_of(j), dsts=[a_of(j) for d in dsts])], local_sem=s.sent)
+
+    home, mate = wc(h, c, 0), wc(h, c ^ 1, 0)
+
+    if l in (2, 3, 6, 7):
+        src_host = h if l < 4 else 1 - h
+        first = 2 if l < 4 else 6
+        n = 0
+        for k in range(l - first, 8, 2):
+            j = blk(src_host, c - 2 * k)
+            g.wait_ge(arr[j], 8)
+            if k == 0 and l == 2:
+                send(j, [mate])
+            elif k == 0:
+                send(j, [home, mate] + [wc(h, c + 2 * q, 6 + q % 2) for q in range(1, 8)])
+            else:
+                send(j, [home, mate])
+            n += 8
+        g.wait_ge(s.sent, n)
+        return
+    if l != 0:
+        return
+
+    me = blk(h, c)
+    g.dma_start(a_of(me), T.a[:]).then_inc(s.lda, 16)
+    g.sync.dma_start(T.wt[:], T.w[:]).then_inc(s.ldw, 16)
+    g.wait_ge(s.lda, 16)
+    send(me, [wc(1 - h, c, 6), wc(h, c, 2)] + [wc(h, c + 2 * q, 2 + q % 2) for q in range(1, 8)])
+    g.wait_ge(s.sent, 8)
+
+    m = c ^ 1
+    order = ([me, blk(1 - h, c)] + [blk(h, c - 2 * k) for k in range(1, 8)] + [blk(h, m)]
+             + [blk(1 - h, c - 2 * k) for k in range(1, 8)] + [blk(1 - h, m)]
+             + [blk(h, m - 2 * k) for k in range(1, 8)] + [blk(1 - h, m - 2 * k) for k in range(1, 8)])
+    n_first = 25
+
+    g.tensor.wait_ge(s.ldw, 16)
+    for i, j in enumerate(order):
+        if j == me:
+            g.tensor.wait_ge(s.lda, 16)
+        else:
+            g.tensor.wait_ge(arr[j], 8)
+        if i >= NBANK:
+            g.tensor.wait_ge(s.cp, i - NBANK + 1)
+        bank = T.acc[:, 512 * (i % NBANK):512 * (i % NBANK) + NO]
+        for t in range(KT):
+            mmi = g.tensor.matmul(bank, T.ag[:, BW * j + 128 * t:BW * j + 128 * (t + 1)],
+                                  T.wt[:, NO * t:NO * (t + 1)], start=(t == 0), stop=(t == KT - 1))
+        mmi.then_inc(s.mm, 1)
+        g.vector.wait_ge(s.mm, i + 1)
+        g.vector.tensor_copy(T.yo[:, NO * j:NO * (j + 1)], bank).then_inc(s.cp, 1)
+
+    lo, hi = 16 * h * NO, 16 * (1 - h) * NO
+    g.sync.wait_ge(s.cp, n_first)
+    g.sync.dma_start(T.y[:, lo:lo + 16 * NO], T.yo[:, lo:lo + 16 * NO]).then_inc(s.st, 16)
+    g.sync.wait_ge(s.cp, NR)
+    g.sync.dma_start(T.y[:, hi:hi + 16 * NO], T.yo[:, hi:hi + 16 * NO]).then_inc(s.st, 16)
+    g.sync.wait_ge(s.st, 32)

@@ -1,96 +1,111 @@
 import concourse.bass as bass
 
 NR, BW, NO, KT = 32, 512, 256, 4
-NBANK = 8
+OWN = 8
 SCRATCH = {
-    "ag": ("sbuf", [128, NR * BW], "bfloat16"),
+    "ag": ("sbuf", [128, 9 * BW], "bfloat16"),
     "wt": ("sbuf", [128, KT * NO], "bfloat16"),
     "yo": ("sbuf", [128, NR * NO], "bfloat16"),
-    "acc": ("psum", [128, NBANK * 512], "float32"),
+    "acc": ("psum", [128, 8 * 512], "float32"),
 }
-SEMAPHORES = ["arr%d" % j for j in range(NR)] + ["lda", "ldw", "sent", "mm", "cp", "st"]
+SEMAPHORES = ["arr0", "arr1", "arr2", "arr3", "arr4", "arr5", "arr6", "arr7",
+              "lda", "ldw", "warr", "sent", "mm", "cp", "ya", "yb", "st"]
 
 OFF = 0x00FF
+ALL = 0xFFFF
 
 
 def rank_program(g, core, T, topo):
     s = T.sem
-    arr = [s.arr0, s.arr1, s.arr2, s.arr3, s.arr4, s.arr5, s.arr6, s.arr7,
-           s.arr8, s.arr9, s.arr10, s.arr11, s.arr12, s.arr13, s.arr14, s.arr15,
-           s.arr16, s.arr17, s.arr18, s.arr19, s.arr20, s.arr21, s.arr22, s.arr23,
-           s.arr24, s.arr25, s.arr26, s.arr27, s.arr28, s.arr29, s.arr30, s.arr31]
+    arr = [s.arr0, s.arr1, s.arr2, s.arr3, s.arr4, s.arr5, s.arr6, s.arr7]
     h, c, l = topo.host(core), topo.chip(core), core % 8
+    plane = [(c - 2 * k) % 16 for k in range(8)]
 
     def wc(hh, cc, ll):
-        return 128 * hh + 8 * (cc % 16) + ll
+        return 128 * hh + 8 * cc + ll
 
-    def blk(hh, cc):
-        return T.rank_of(wc(hh, cc, 0))
+    def slot(i):
+        return T.ag[:, BW * i:BW * (i + 1)]
 
-    def a_of(j):
-        return T.ag[:, BW * j:BW * (j + 1)]
-
-    def send(j, dsts):
-        ids = []
+    def ids(dsts):
+        out = []
         for d in dsts:
             rid, pid = topo.addr(d, core)
-            ids.append(bass.DstId(rid=rid, pnc=pid))
-        g.remote_dma_fused([bass.RemoteDMATransfer(dst_ids=ids, dma_engine_mask=OFF, remote_sem=arr[j],
-                                                   src=a_of(j), dsts=[a_of(j) for d in dsts])], local_sem=s.sent)
+            out.append(bass.DstId(rid=rid, pnc=pid))
+        return out
 
-    home, mate = wc(h, c, 0), wc(h, c ^ 1, 0)
+    def send(src, dst, dsts):
+        g.remote_dma_fused([bass.RemoteDMATransfer(dst_ids=ids(dsts), dma_engine_mask=OFF, remote_sem=arr[dst],
+                                                   src=slot(src), dsts=[slot(dst) for d in dsts])], local_sem=s.sent)
 
-    if l in (2, 3, 6, 7):
-        src_host = h if l < 4 else 1 - h
-        first = 2 if l < 4 else 6
-        n = 0
-        for k in range(l - first, 8, 2):
-            j = blk(src_host, c - 2 * k)
-            g.wait_ge(arr[j], 8)
-            if k == 0 and l == 2:
-                send(j, [mate])
-            elif k == 0:
-                send(j, [home, mate] + [wc(h, c + 2 * q, 6 + q % 2) for q in range(1, 8)])
+    def multiply(todo):
+        for i, (sl, j) in enumerate(todo):
+            g.tensor.wait_ge(arr[sl], 8)
+            bank = T.acc[:, 512 * i:512 * i + NO]
+            for t in range(KT):
+                mmi = g.tensor.matmul(bank, T.ag[:, BW * sl + 128 * t:BW * sl + 128 * (t + 1)],
+                                      T.wt[:, NO * t:NO * (t + 1)], start=(t == 0), stop=(t == KT - 1))
+            mmi.then_inc(s.mm, 1)
+            g.vector.wait_ge(s.mm, i + 1)
+            g.vector.tensor_copy(T.yo[:, NO * j:NO * (j + 1)], bank).then_inc(s.cp, 1)
+
+    if l == 0:
+        g.dma_start(slot(OWN), T.a[:]).then_inc(s.lda, 16)
+        g.sync.dma_start(T.wt[:], T.w[:]).then_inc(s.ldw, 16)
+        g.wait_ge(s.lda, 16)
+        send(OWN, (c % 8) // 2, [wc(1 - h, c, 4)] + [wc(h, x, 2 + c // 8) for x in plane])
+        g.wait_ge(s.ldw, 16)
+        rid, pid = topo.addr(wc(h, c, 1), core)
+        g.remote_dma(T.wt[:], T.wt[:], s.warr, s.sent, pid, rid, ALL)
+        g.wait_ge(s.sent, 8 + 16)
+        g.tensor.wait_ge(s.ldw, 16)
+        multiply([((x ^ 1) // 2, T.rank_of(wc(1 - h, x ^ 1, 0))) for x in plane])
+        lo, hi = 16 * h * NO, 16 * (1 - h) * NO
+        g.sync.wait_ge(s.ya, 32)
+        g.sync.dma_start(T.y[:, lo:lo + 16 * NO], T.yo[:, lo:lo + 16 * NO]).then_inc(s.st, 16)
+        g.sync.wait_ge(s.yb, 32)
+        g.sync.wait_ge(s.cp, 8)
+        g.sync.dma_start(T.y[:, hi:hi + 16 * NO], T.yo[:, hi:hi + 16 * NO]).then_inc(s.st, 16)
+        g.sync.wait_ge(s.st, 32)
+
+    elif l == 1:
+        g.wait_ge(s.warr, 16)
+        dsts = [wc(h, c, x) for x in (2, 3, 6, 7)]
+        g.remote_dma_fused([bass.RemoteDMATransfer(dst_ids=ids(dsts), dma_engine_mask=ALL, remote_sem=s.warr,
+                                                   src=T.wt[:], dsts=[T.wt[:] for d in dsts])], local_sem=s.sent)
+        g.wait_ge(s.sent, 16)
+
+    elif l == 4:
+        sl = (c % 8) // 2
+        g.wait_ge(arr[sl], 8)
+        send(sl, sl, [wc(h, x, 6 + c // 8) for x in plane])
+        g.wait_ge(s.sent, 8)
+
+    elif l in (2, 3, 6, 7):
+        u = l % 2
+        mine = [x for x in plane if x // 8 == u]
+        home = wc(h, c, 0)
+        for x in mine:
+            sl = (x % 8) // 2
+            g.wait_ge(arr[sl], 8)
+            if l < 4:
+                send(sl, 4 + sl, [wc(h, c ^ 1, l)])
             else:
-                send(j, [home, mate])
-            n += 8
-        g.wait_ge(s.sent, n)
-        return
-    if l != 0:
-        return
-
-    me = blk(h, c)
-    g.dma_start(a_of(me), T.a[:]).then_inc(s.lda, 16)
-    g.sync.dma_start(T.wt[:], T.w[:]).then_inc(s.ldw, 16)
-    g.wait_ge(s.lda, 16)
-    send(me, [wc(1 - h, c, 6), wc(h, c, 2)] + [wc(h, c + 2 * q, 2 + q % 2) for q in range(1, 8)])
-    g.wait_ge(s.sent, 8)
-
-    m = c ^ 1
-    order = ([me, blk(1 - h, c)] + [blk(h, c - 2 * k) for k in range(1, 8)] + [blk(h, m)]
-             + [blk(1 - h, c - 2 * k) for k in range(1, 8)] + [blk(1 - h, m)]
-             + [blk(h, m - 2 * k) for k in range(1, 8)] + [blk(1 - h, m - 2 * k) for k in range(1, 8)])
-    n_first = 25
-
-    g.tensor.wait_ge(s.ldw, 16)
-    for i, j in enumerate(order):
-        if j == me:
-            g.tensor.wait_ge(s.lda, 16)
+                send(sl, x // 2, [wc(h, c ^ 1, 0)])
+        g.tensor.wait_ge(s.warr, 16)
+        if l < 4:
+            multiply([((x % 8) // 2, T.rank_of(wc(h, x, 0))) for x in mine]
+                     + [(4 + (x % 8) // 2, T.rank_of(wc(h, x ^ 1, 0))) for x in mine])
+            g.wait_ge(s.cp, 8)
+            lo = (16 * h + 8 * u) * NO
+            rid, pid = topo.addr(home, core)
+            g.remote_dma(T.yo[:, lo:lo + 8 * NO], T.yo[:, lo:lo + 8 * NO], s.ya, s.sent, pid, rid, ALL)
+            g.wait_ge(s.sent, 32 + 16)
         else:
-            g.tensor.wait_ge(arr[j], 8)
-        if i >= NBANK:
-            g.tensor.wait_ge(s.cp, i - NBANK + 1)
-        bank = T.acc[:, 512 * (i % NBANK):512 * (i % NBANK) + NO]
-        for t in range(KT):
-            mmi = g.tensor.matmul(bank, T.ag[:, BW * j + 128 * t:BW * j + 128 * (t + 1)],
-                                  T.wt[:, NO * t:NO * (t + 1)], start=(t == 0), stop=(t == KT - 1))
-        mmi.then_inc(s.mm, 1)
-        g.vector.wait_ge(s.mm, i + 1)
-        g.vector.tensor_copy(T.yo[:, NO * j:NO * (j + 1)], bank).then_inc(s.cp, 1)
-
-    lo, hi = 16 * h * NO, 16 * (1 - h) * NO
-    g.sync.wait_ge(s.cp, n_first)
-    g.sync.dma_start(T.y[:, lo:lo + 16 * NO], T.yo[:, lo:lo + 16 * NO]).then_inc(s.st, 16)
-    g.sync.wait_ge(s.cp, NR)
-    g.sync.dma_start(T.y[:, hi:hi + 16 * NO], T.yo[:, hi:hi + 16 * NO]).then_inc(s.st, 16)
-    g.sync.wait_ge(s.st, 32)
+            ranks = [T.rank_of(wc(1 - h, x, 0)) for x in mine]
+            multiply([((x % 8) // 2, j) for x, j in zip(mine, ranks)])
+            g.wait_ge(s.cp, 4)
+            g.remote_dma_fused([bass.RemoteDMATransfer(dst_ids=ids([home]), dma_engine_mask=0xF << (4 * i), remote_sem=s.yb,
+                                                       src=T.yo[:, NO * j:NO * (j + 1)], dst=T.yo[:, NO * j:NO * (j + 1)])
+                                for i, j in enumerate(ranks)], local_sem=s.sent)
+            g.wait_ge(s.sent, 32 + 16)

import concourse.bass as bass

NR, BW, NO, KT = 32, 512, 256, 4
OWN = 8
SCRATCH = {
    "ag": ("sbuf", [128, 9 * BW], "bfloat16"),
    "wt": ("sbuf", [128, KT * NO], "bfloat16"),
    "yo": ("sbuf", [128, NR * NO], "bfloat16"),
    "acc": ("psum", [128, 8 * 512], "float32"),
}
SEMAPHORES = ["arr0", "arr1", "arr2", "arr3", "arr4", "arr5", "arr6", "arr7",
              "lda", "ldw", "warr", "sent", "mm", "cp", "ya", "yb", "st"]

OFF = 0x00FF
ALL = 0xFFFF


def rank_program(g, core, T, topo):
    s = T.sem
    arr = [s.arr0, s.arr1, s.arr2, s.arr3, s.arr4, s.arr5, s.arr6, s.arr7]
    h, c, l = topo.host(core), topo.chip(core), core % 8
    plane = [(c - 2 * k) % 16 for k in range(8)]

    def wc(hh, cc, ll):
        return 128 * hh + 8 * cc + ll

    def slot(i):
        return T.ag[:, BW * i:BW * (i + 1)]

    def ids(dsts):
        out = []
        for d in dsts:
            rid, pid = topo.addr(d, core)
            out.append(bass.DstId(rid=rid, pnc=pid))
        return out

    def send(src, dst, dsts):
        g.remote_dma_fused([bass.RemoteDMATransfer(dst_ids=ids(dsts), dma_engine_mask=OFF, remote_sem=arr[dst],
                                                   src=slot(src), dsts=[slot(dst) for d in dsts])], local_sem=s.sent)

    def multiply(todo):
        for i, (sl, j) in enumerate(todo):
            g.tensor.wait_ge(arr[sl], 8)
            bank = T.acc[:, 512 * i:512 * i + NO]
            for t in range(KT):
                mmi = g.tensor.matmul(bank, T.ag[:, BW * sl + 128 * t:BW * sl + 128 * (t + 1)],
                                      T.wt[:, NO * t:NO * (t + 1)], start=(t == 0), stop=(t == KT - 1))
            mmi.then_inc(s.mm, 1)
            g.vector.wait_ge(s.mm, i + 1)
            g.vector.tensor_copy(T.yo[:, NO * j:NO * (j + 1)], bank).then_inc(s.cp, 1)

    if l == 0:
        g.dma_start(slot(OWN), T.a[:]).then_inc(s.lda, 16)
        g.sync.dma_start(T.wt[:], T.w[:]).then_inc(s.ldw, 16)
        g.wait_ge(s.lda, 16)
        send(OWN, (c % 8) // 2, [wc(1 - h, c, 4)] + [wc(h, x, 2 + c // 8) for x in plane])
        g.wait_ge(s.ldw, 16)
        rid, pid = topo.addr(wc(h, c, 1), core)
        g.remote_dma(T.wt[:], T.wt[:], s.warr, s.sent, pid, rid, ALL)
        g.wait_ge(s.sent, 8 + 16)
        g.tensor.wait_ge(s.ldw, 16)
        multiply([((x ^ 1) // 2, T.rank_of(wc(1 - h, x ^ 1, 0))) for x in plane])
        lo, hi = 16 * h * NO, 16 * (1 - h) * NO
        g.sync.wait_ge(s.ya, 32)
        g.sync.dma_start(T.y[:, lo:lo + 16 * NO], T.yo[:, lo:lo + 16 * NO]).then_inc(s.st, 16)
        g.sync.wait_ge(s.yb, 32)
        g.sync.wait_ge(s.cp, 8)
        g.sync.dma_start(T.y[:, hi:hi + 16 * NO], T.yo[:, hi:hi + 16 * NO]).then_inc(s.st, 16)
        g.sync.wait_ge(s.st, 32)

    elif l == 1:
        g.wait_ge(s.warr, 16)
        dsts = [wc(h, c, x) for x in (2, 3, 6, 7)]
        g.remote_dma_fused([bass.RemoteDMATransfer(dst_ids=ids(dsts), dma_engine_mask=ALL, remote_sem=s.warr,
                                                   src=T.wt[:], dsts=[T.wt[:] for d in dsts])], local_sem=s.sent)
        g.wait_ge(s.sent, 16)

    elif l == 4:
        sl = (c % 8) // 2
        g.wait_ge(arr[sl], 8)
        send(sl, sl, [wc(h, x, 6 + c // 8) for x in plane])
        g.wait_ge(s.sent, 8)

    elif l in (2, 3, 6, 7):
        u = l % 2
        mine = [x for x in plane if x // 8 == u]
        home = wc(h, c, 0)
        for x in mine:
            sl = (x % 8) // 2
            g.wait_ge(arr[sl], 8)
            if l < 4:
                send(sl, 4 + sl, [wc(h, c ^ 1, l)])
            else:
                send(sl, x // 2, [wc(h, c ^ 1, 0)])
        g.tensor.wait_ge(s.warr, 16)
        if l < 4:
            multiply([((x % 8) // 2, T.rank_of(wc(h, x, 0))) for x in mine]
                     + [(4 + (x % 8) // 2, T.rank_of(wc(h, x ^ 1, 0))) for x in mine])
            g.wait_ge(s.cp, 8)
            lo = (16 * h + 8 * u) * NO
            rid, pid = topo.addr(home, core)
            g.remote_dma(T.yo[:, lo:lo + 8 * NO], T.yo[:, lo:lo + 8 * NO], s.ya, s.sent, pid, rid, ALL)
            g.wait_ge(s.sent, 32 + 16)
        else:
            ranks = [T.rank_of(wc(1 - h, x, 0)) for x in mine]
            multiply([((x % 8) // 2, j) for x, j in zip(mine, ranks)])
            g.wait_ge(s.cp, 4)
            g.remote_dma_fused([bass.RemoteDMATransfer(dst_ids=ids([home]), dma_engine_mask=0xF << (4 * i), remote_sem=s.yb,
                                                       src=T.yo[:, NO * j:NO * (j + 1)], dst=T.yo[:, NO * j:NO * (j + 1)])
                                for i, j in enumerate(ranks)], local_sem=s.sent)
            g.wait_ge(s.sent, 32 + 16)
